import numpy as np
import ml_dtypes


def mxq(x, axis, fmt="e4m3"):
    dtype, down = {"e4m3": (ml_dtypes.float8_e4m3fn, 7), "e5m2": (ml_dtypes.float8_e5m2, 14)}[fmt]
    v = np.moveaxis(np.asarray(x, np.float32).astype(ml_dtypes.bfloat16).astype(np.float64), axis, -1)
    blocks = v.reshape(v.shape[:-1] + (-1, 32))
    amax = np.abs(blocks).max(-1, keepdims=True)
    byte = np.maximum(np.where(amax > 0, np.frexp(amax)[1] - 1 + 127, 0) - down, 1)
    scale = np.exp2(byte - 127.0)
    codes = (blocks / scale).astype(np.float32).astype(dtype).astype(np.float64)
    return np.moveaxis((codes * scale).reshape(v.shape), -1, axis)


WIDE = False


def mx_kscale(k):
    if not WIDE:
        return np.ones(k)
    levels = np.array([10, -10, 5, -5, 0])
    if k % 512:
        return np.exp2(np.random.permutation(np.resize(levels, k // 32))).repeat(32)
    a = np.empty((k // 512, 16))
    for p in range(k // 512):
        a[p, :8] = np.random.permutation(np.resize(levels, 8))
        for g in range(8):
            far = levels[np.abs(levels - a[p, g]) >= 10]
            a[p, g + 8] = far[np.random.randint(len(far))]
    return np.exp2(a.ravel()).repeat(32)


def f64(x):
    return np.asarray(x).astype(np.float64)


def striped(idx):
    return np.tile(idx.reshape(-1, 16).T, (8, 1)).astype(np.uint16)


def unstriped(offs):
    return offs[:16].T.reshape(-1).astype(np.int64)


def pack_weight(w):
    k, n = w.shape
    w = f64(np.asarray(w, np.float32).astype(ml_dtypes.bfloat16)).reshape(k // 32, 32, n)
    amax = np.abs(w).max(1)
    byte = np.clip(np.where(amax > 0, np.frexp(amax)[1] - 1 + 127 - 7, 1), 1, 254)
    scaled = (w * np.exp2(127.0 - byte)[:, None, :]).reshape(k, n).astype(np.float32)
    words = np.ascontiguousarray(scaled.reshape(k // 512, 128, 4, n).transpose(0, 1, 3, 2)).astype(ml_dtypes.float8_e4m3fn).view(np.uint8)
    return words, np.ascontiguousarray(byte.astype(np.uint8).reshape(k // 512, 16, n))


def unpack_weight(words, scales):
    g, p, n, _ = words.shape
    vals = np.ascontiguousarray(words).view(ml_dtypes.float8_e4m3fn).astype(np.float64) * np.repeat(np.exp2(scales.astype(np.float64) - 127.0), 8, axis=1)[..., None]
    return vals.transpose(0, 1, 3, 2).reshape(g * 512, n)


def relu2(v):
    return np.maximum(v, 0.0) ** 2


K, T, E, C, N = 1024, 1536, 24, 128, 128


def by_expert(wq, xq):
    return np.concatenate([wq[e].T @ xq[:, e * C:(e + 1) * C] for e in range(E)], axis=1)


def setup_inputs():
    n = np.random.standard_normal
    s = mx_kscale(K)[:, None]
    first = np.random.permutation(np.repeat(np.arange(E), T // E))
    second = (first + 1 + np.random.permutation(np.repeat(np.arange(E - 1), -(-T // (E - 1)))[:T])) % E
    while np.bincount(second, minlength=E).max() != T // E:
        load = np.bincount(second, minlength=E); hi, lo = int(load.argmax()), int(load.argmin())
        t = np.flatnonzero((second == hi) & (first != lo))[0]; second[t] = lo
    slot_token = np.empty(E * C, np.int64); pos = np.empty((2, T), np.int64); fill = np.zeros(E, np.int64)
    place = np.stack([np.random.permutation(C) for _ in range(E)])
    for r, deal in enumerate((first, second)):
        for t in np.random.permutation(T):
            e = deal[t]; j = e * C + place[e, fill[e]]; fill[e] += 1; slot_token[j] = t; pos[r, t] = j
    g = np.random.uniform(0.2, 0.8, T)
    packed = [pack_weight(m) for m in n((E, K, N)) / np.sqrt(K) / s[None]]
    return {
        "xT": (n((K, T)) * s).astype(np.float32),
        "w_words": np.stack([m[0] for m in packed]),
        "w_scales": np.stack([m[1] for m in packed]),
        "b": (0.3 * n((N, E))).astype(np.float32),
        "gate": np.stack([np.tile(g, (N, 1)), np.tile(1.0 - g, (N, 1))]).astype(np.float32),
        "offs": striped(slot_token),
        "pos1": striped(pos[0]),
        "pos2": striped(pos[1]),
    }


def reference(xT, w_words, w_scales, b, gate, offs, pos1, pos2):
    idx = unstriped(offs)
    xq = mxq(f64(xT)[:, idx], 0, "e4m3")
    w = np.stack([unpack_weight(w_words[e], w_scales[e]) for e in range(E)])
    y = by_expert(w, xq)
    y = relu2(y + np.repeat(f64(b), C, axis=1))
    return f64(gate[0]) * y[:, unstriped(pos1)] + f64(gate[1]) * y[:, unstriped(pos2)]

@@ -1,0 +1,195 @@
+from contextlib import ExitStack
+
+import concourse.mybir as mybir
+from concourse.masks import make_identity
+
+FLOPS = 805306368
+
+F32 = mybir.dt.float32
+BF16 = mybir.dt.bfloat16
+I32 = mybir.dt.int32
+U32 = mybir.dt.uint32
+U16 = mybir.dt.uint16
+U8 = mybir.dt.uint8
+FP8X4 = mybir.dt.float8_e4m3fn_x4
+Relu = mybir.ActivationFunctionType.Relu
+Square = mybir.ActivationFunctionType.Square
+mult = mybir.AluOpType.mult
+add = mybir.AluOpType.add
+Max = mybir.AluOpType.max
+
+P = 128
+T = 1536
+E = 24
+C = 128
+S = E * C
+UNITS = [
+    (0, 512, ((512, ((320, "v"), (192, "s"))),)),
+    (0, 512, ((512, ((320, "v"), (192, "s"))),)),
+    (0, 256, ((256, ((160, "v"), (96, "s"))),)),
+    (0, 256, ((256, ((160, "v"), (96, "s"))),)),
+    (1, 512, ((512, ((256, "s"), (256, "s"))),)),
+    (1, 512, ((512, ((256, "s"), (256, "s"))),)),
+    (1, 256, ((256, ((256, "s"),)),)),
+    (1, 256, ((256, ((256, "s"),)),)),
+]
+WORD0 = [1024, 1024, 1024]
+STEPS = [
+    ("b", 512), ("w", 512), ("b", 512), ("w", 512), ("b", 1024), ("w", 1024), ("b", 512), ("w", 512), ("b", 512), ("w", 256), ("w", 256),
+]
+LOADS = [4, 8, 12]
+COMBINE = [(512, "pe", (512,)), (512, "v", (512,)), (512, "v", (256, 256))]
+
+
+def tile_routed_moe_kernel(tc, xT, w_words, w_scales, b, gate, offs, pos1, pos2, out):
+    nc = tc.nc
+    with ExitStack() as ctx:
+        keep = ctx.enter_context(tc.tile_pool(name="keep", bufs=1))
+        psum = ctx.enter_context(tc.psum_pool(name="psum", bufs=1))
+
+        offs_t = keep.tile([P, S // 16], U16, name="offs_t")
+        pos1_t = keep.tile([P, T // 16], U16, name="pos1_t")
+        pos2_t = keep.tile([P, T // 16], U16, name="pos2_t")
+        codes = [keep.tile([P, T], U32, name=f"codes{a}", align_bytes=64) for a in range(2)]
+        scales = keep.tile([P, T], U8, name="scales", align_bytes=64)
+        g_codes = [keep.tile([P, S], U32, name=f"g_codes{a}", align_bytes=64) for a in range(2)]
+        g_scales = keep.tile([P, S], U8, name="g_scales", align_bytes=64)
+        w_codes = keep.tile([P, E, 2, C], U32, name="w_codes", align_bytes=64)
+        w_planes = keep.tile([P, S], U8, name="w_planes", align_bytes=64)
+        bias = keep.tile([P, E], F32, name="bias")
+        relu = keep.tile([P, S], F32, name="relu")
+        ys = keep.tile([P, S], F32, name="ys")
+        gates = keep.tile([P, 2, T], F32, name="gates")
+
+        nc.gpsimd.memset(scales[:], 0)
+        nc.gpsimd.memset(w_planes[:].bitcast(I32), 0)
+        ident = keep.tile([P, P], F32, name="ident")
+        make_identity(nc, ident[:])
+
+        x_view = xT.rearrange("(a p j) t -> a p j t", p=P, j=4)
+        grouped = []
+        starts = []
+        first = {0: 0, 1: 0}
+        for i, (a, n, parts) in enumerate(UNITS):
+            g = keep.tile([P, n, 4], BF16, name=f"grouped{i}", align_bytes=64)
+            u0 = 0
+            for k, (m, copies) in enumerate(parts):
+                t0 = first[a] + u0
+                raw = keep.tile([P, 4, m], F32, name=f"raw{i}_{k}")
+                nc.sync.dma_start(out=raw[:], in_=x_view[a, :, :, t0 : t0 + m])
+                c0 = 0
+                for c, eng in copies:
+                    src = raw[:, :, c0 : c0 + c].rearrange("p j t -> p t j")
+                    if eng == "v":
+                        nc.vector.tensor_copy(out=g[:, u0 + c0 : u0 + c0 + c, :], in_=src)
+                    else:
+                        nc.scalar.copy(out=g[:, u0 + c0 : u0 + c0 + c, :], in_=src)
+                    c0 += c
+                u0 += m
+            if i == 3:
+                nc.sync.dma_start(offs_t[:], offs)
+            grouped.append(g)
+            starts.append(first[a])
+            first[a] += n
+        nc.sync.dma_start(out=bias[:], in_=b)
+        for a in range(2):
+            for q in range(4):
+                row = 32 * q + 4 * a
+                nc.sync.dma_start(
+                    out=w_planes[row : row + 4, :].bitcast(I32).rearrange("q (e n) -> q e n", e=E),
+                    in_=w_scales[:, a, 4 * q : 4 * q + 4, :].rearrange("e q n -> q e n").bitcast(I32),
+                )
+        e0 = 0
+        for n in LOADS:
+            nc.sync.dma_start(
+                out=w_codes[:, e0 : e0 + n, :, :].bitcast(I32),
+                in_=w_words[e0 : e0 + n].rearrange("e a p n r -> p e a (n r)").bitcast(I32),
+            )
+            e0 += n
+        nc.sync.dma_start(pos1_t[:], pos1)
+        nc.sync.dma_start(pos2_t[:], pos2)
+        nc.sync.dma_start(out=gates[:], in_=gate.rearrange("r p t -> p r t"))
+
+        def quantise(i):
+            a, n, parts = UNITS[i]
+            t0 = starts[i]
+            nc.vector.quantize_mx(
+                out=codes[a][:, t0 : t0 + n].bitcast(FP8X4),
+                scales=scales[4 * a : P, t0 : t0 + n],
+                in_=grouped[i][:].rearrange("p t j -> p (t j)"),
+            )
+
+        def gather(dst, src, s0, n):
+            nc.vector.tensor_copy(dst[:, s0 : s0 + n], src[:].indirect(offs_t[:, s0 // 16 : (s0 + n) // 16]))
+
+        for i in range(len(UNITS)):
+            if UNITS[i][0] == 0:
+                quantise(i)
+        s0 = 0
+        for n in WORD0:
+            gather(g_codes[0], codes[0], s0, n)
+            s0 += n
+        for i in range(len(UNITS)):
+            if UNITS[i][0] == 1:
+                quantise(i)
+
+        done = {"b": 0, "w": 0}
+        banks = {}
+        for sort, n in STEPS:
+            s0 = done[sort]
+            done[sort] += n
+            if sort == "b":
+                gather(g_scales, scales, s0, n)
+                continue
+            gather(g_codes[1], codes[1], s0, n)
+            for e in range(s0 // C, (s0 + n) // C):
+                cols = slice(e * C, (e + 1) * C)
+                if e % 4 == 0:
+                    banks[e // 4] = psum.tile([P, 4 * C], F32, name=f"bank{e // 4}")
+                acc = banks[e // 4][:, (e % 4) * C : (e % 4 + 1) * C]
+                for a in range(2):
+                    nc.tensor.matmul_mx(
+                        out=acc,
+                        lhsT=w_codes[:, e, a, :].bitcast(FP8X4),
+                        lhsT_scale=w_planes[4 * a : P, cols],
+                        rhs=g_codes[a][:, cols].bitcast(FP8X4),
+                        rhs_scale=g_scales[4 * a : P, cols],
+                        start=(a == 0),
+                        stop=(a == 1),
+                    )
+                if e == E - 1:
+                    nc.vector.tensor_scalar(relu[:, cols], acc, bias[:, e : e + 1], 0.0, add, Max)
+                    nc.vector.tensor_tensor(ys[:, cols], relu[:, cols], relu[:, cols], mult)
+                else:
+                    nc.scalar.activation(relu[:, cols], acc, Relu, bias=bias[:, e : e + 1])
+                    if e == E - 2:
+                        nc.scalar.activation(ys[:, cols], relu[:, cols], Square)
+            for c0 in range(s0, s0 + n, 512):
+                c1 = min(c0 + 512, s0 + n)
+                if s0 + n == S:
+                    continue
+                nc.gpsimd.tensor_tensor(ys[:, c0:c1], relu[:, c0:c1], relu[:, c0:c1], mult)
+
+        t0 = 0
+        for i, (n, how, stores) in enumerate(COMBINE):
+            parts = []
+            for r, pos in enumerate((pos1_t, pos2_t)):
+                part = keep.tile([P, n], F32, name=f"part{i}_{r}")
+                nc.vector.tensor_tensor(
+                    part[:], ys[:].indirect(pos[:, t0 // 16 : (t0 + n) // 16]), gates[:, r, t0 : t0 + n], mult
+                )
+                parts.append(part)
+            if how == "pe":
+                both = psum.tile([P, n], F32, name=f"both{i}")
+                for r in range(2):
+                    nc.tensor.matmul(both[:], ident[:], parts[r][:], start=(r == 0), stop=(r == 1))
+            u0 = 0
+            for k, m in enumerate(stores):
+                total = keep.tile([P, m], F32, name=f"total{i}_{k}")
+                if how == "pe":
+                    nc.scalar.copy(out=total[:], in_=both[:, u0 : u0 + m])
+                else:
+                    nc.vector.tensor_tensor(total[:], parts[0][:, u0 : u0 + m], parts[1][:, u0 : u0 + m], add)
+                nc.sync.dma_start(out=out[:, t0 + u0 : t0 + u0 + m], in_=total[:])
+                u0 += m
+            t0 += n

@@ -23,21 +23,15 @@ T = 1536
 E = 24
 C = 128
 S = E * C
-UNITS = [
-    (0, 512, ((512, ((320, "v"), (192, "s"))),)),
-    (0, 512, ((512, ((320, "v"), (192, "s"))),)),
-    (0, 256, ((256, ((160, "v"), (96, "s"))),)),
-    (0, 256, ((256, ((160, "v"), (96, "s"))),)),
-    (1, 512, ((512, ((256, "s"), (256, "s"))),)),
-    (1, 512, ((512, ((256, "s"), (256, "s"))),)),
-    (1, 256, ((256, ((256, "s"),)),)),
-    (1, 256, ((256, ((256, "s"),)),)),
+X_COPIES = [
+    [(256, "v"), (256, "s"), (256, "v"), (320, "v"), (192, "s"), (160, "v"), (96, "s")],
+    [(256, "s")] * 6,
 ]
+X_QUANT = [[512, 512, 256, 256], [512, 512, 256, 256]]
 WORD0 = [1024, 1024, 1024]
 STEPS = [
     ("b", 512), ("w", 512), ("b", 512), ("w", 512), ("b", 1024), ("w", 1024), ("b", 512), ("w", 512), ("b", 512), ("w", 256), ("w", 256),
 ]
-LOADS = [4, 8, 12]
 COMBINE = [(512, "pe", (512,)), (512, "v", (512,)), (512, "v", (256, 256))]
 
 
@@ -67,71 +61,77 @@ def tile_routed_moe_kernel(tc, xT, w_words, w_scales, b, gate, offs, pos1, pos2,
         make_identity(nc, ident[:])
 
         x_view = xT.rearrange("(a p j) t -> a p j t", p=P, j=4)
-        grouped = []
-        starts = []
-        first = {0: 0, 1: 0}
-        for i, (a, n, parts) in enumerate(UNITS):
-            g = keep.tile([P, n, 4], BF16, name=f"grouped{i}", align_bytes=64)
-            u0 = 0
-            for k, (m, copies) in enumerate(parts):
-                t0 = first[a] + u0
-                raw = keep.tile([P, 4, m], F32, name=f"raw{i}_{k}")
-                nc.sync.dma_start(out=raw[:], in_=x_view[a, :, :, t0 : t0 + m])
-                c0 = 0
-                for c, eng in copies:
-                    src = raw[:, :, c0 : c0 + c].rearrange("p j t -> p t j")
-                    if eng == "v":
-                        nc.vector.tensor_copy(out=g[:, u0 + c0 : u0 + c0 + c, :], in_=src)
-                    else:
-                        nc.scalar.copy(out=g[:, u0 + c0 : u0 + c0 + c, :], in_=src)
-                    c0 += c
-                u0 += m
-            if i == 3:
-                nc.sync.dma_start(offs_t[:], offs)
-            grouped.append(g)
-            starts.append(first[a])
-            first[a] += n
-        nc.sync.dma_start(out=bias[:], in_=b)
-        for a in range(2):
-            for q in range(4):
-                row = 32 * q + 4 * a
-                nc.sync.dma_start(
-                    out=w_planes[row : row + 4, :].bitcast(I32).rearrange("q (e n) -> q e n", e=E),
-                    in_=w_scales[:, a, 4 * q : 4 * q + 4, :].rearrange("e q n -> q e n").bitcast(I32),
-                )
-        e0 = 0
-        for n in LOADS:
+        raw_of = [[], []]
+
+        def load_x(a, t0, n):
+            raw = keep.tile([P, 4, n], F32, name=f"raw{a}_{t0}")
+            nc.sync.dma_start(out=raw[:], in_=x_view[a, :, :, t0 : t0 + n])
+            raw_of[a].append((t0, n, raw))
+
+        def load_scales(i):
+            a, q = i // 4, i % 4
+            row = 32 * q + 4 * a
+            nc.sync.dma_start(
+                out=w_planes[row : row + 4, :].bitcast(I32).rearrange("q (e n) -> q e n", e=E),
+                in_=w_scales[:, a, 4 * q : 4 * q + 4, :].rearrange("e q n -> q e n").bitcast(I32),
+            )
+
+        def load_w(e0, n):
             nc.sync.dma_start(
                 out=w_codes[:, e0 : e0 + n, :, :].bitcast(I32),
                 in_=w_words[e0 : e0 + n].rearrange("e a p n r -> p e a (n r)").bitcast(I32),
             )
-            e0 += n
+
+        load_x(0, 0, 768)
+        load_x(0, 768, 512)
+        load_x(0, 1280, 256)
+        nc.sync.dma_start(offs_t[:], offs)
+        load_x(1, 0, 768)
+        for i in range(4):
+            load_scales(i)
+        load_x(1, 768, 768)
+        for i in range(4, 8):
+            load_scales(i)
+        load_w(0, 4)
+        load_w(4, 4)
+        nc.sync.dma_start(out=bias[:], in_=b)
+        load_w(8, 8)
         nc.sync.dma_start(pos1_t[:], pos1)
         nc.sync.dma_start(pos2_t[:], pos2)
+        load_w(16, 8)
         nc.sync.dma_start(out=gates[:], in_=gate.rearrange("r p t -> p r t"))
 
-        def quantise(i):
-            a, n, parts = UNITS[i]
-            t0 = starts[i]
-            nc.vector.quantize_mx(
-                out=codes[a][:, t0 : t0 + n].bitcast(FP8X4),
-                scales=scales[4 * a : P, t0 : t0 + n],
-                in_=grouped[i][:].rearrange("p t j -> p (t j)"),
-            )
+        grouped = [keep.tile([P, T, 4], BF16, name=f"grouped{a}", align_bytes=64) for a in range(2)]
+        for a in range(2):
+            t0 = 0
+            for n, eng in X_COPIES[a]:
+                l0, ln, raw = [r for r in raw_of[a] if r[0] <= t0 < r[0] + r[1]][0]
+                src = raw[:, :, t0 - l0 : t0 - l0 + n].rearrange("p j t -> p t j")
+                if eng == "v":
+                    nc.vector.tensor_copy(out=grouped[a][:, t0 : t0 + n, :], in_=src)
+                else:
+                    nc.scalar.copy(out=grouped[a][:, t0 : t0 + n, :], in_=src)
+                t0 += n
+
+        def quantise(a):
+            t0 = 0
+            for n in X_QUANT[a]:
+                nc.vector.quantize_mx(
+                    out=codes[a][:, t0 : t0 + n].bitcast(FP8X4),
+                    scales=scales[4 * a : P, t0 : t0 + n],
+                    in_=grouped[a][:, t0 : t0 + n, :].rearrange("p t j -> p (t j)"),
+                )
+                t0 += n
 
         def gather(dst, src, s0, n):
             nc.vector.tensor_copy(dst[:, s0 : s0 + n], src[:].indirect(offs_t[:, s0 // 16 : (s0 + n) // 16]))
 
-        for i in range(len(UNITS)):
-            if UNITS[i][0] == 0:
-                quantise(i)
+        quantise(0)
         s0 = 0
         for n in WORD0:
             gather(g_codes[0], codes[0], s0, n)
             s0 += n
-        for i in range(len(UNITS)):
-            if UNITS[i][0] == 1:
-                quantise(i)
+        quantise(1)
 
         done = {"b": 0, "w": 0}
         banks = {}
@@ -168,7 +168,7 @@ def tile_routed_moe_kernel(tc, xT, w_words, w_scales, b, gate, offs, pos1, pos2,
                 c1 = min(c0 + 512, s0 + n)
                 if s0 + n == S:
                     continue
-                nc.gpsimd.tensor_tensor(ys[:, c0:c1], relu[:, c0:c1], relu[:, c0:c1], mult)
+                nc.scalar.activation(ys[:, c0:c1], relu[:, c0:c1], Square)
 
         t0 = 0
         for i, (n, how, stores) in enumerate(COMBINE):

@@ -25,14 +25,15 @@ C = 128
 S = E * C
 X_COPIES = [
     [(256, "v"), (256, "s"), (256, "v"), (320, "v"), (192, "s"), (160, "v"), (96, "s")],
-    [(256, "s")] * 6,
+    [(512, "s"), (512, "s"), (320, "s"), (192, "v")],
 ]
-X_QUANT = [[512, 512, 256, 256], [512, 512, 256, 256]]
+X_QUANT = [[512, 512, 256, 256], [512, 512, 512]]
 WORD0 = [1024, 1024, 1024]
 STEPS = [
     ("b", 512), ("w", 512), ("b", 512), ("w", 512), ("b", 1024), ("w", 1024), ("b", 512), ("w", 512), ("b", 512), ("w", 256), ("w", 256),
 ]
-COMBINE = [(512, "pe", (512,)), (512, "v", (512,)), (512, "v", (256, 256))]
+PE_TOKENS = 512
+COMBINE = [640, 384]
 
 
 def tile_routed_moe_kernel(tc, xT, w_words, w_scales, b, gate, offs, pos1, pos2, out):
@@ -86,31 +87,30 @@ def tile_routed_moe_kernel(tc, xT, w_words, w_scales, b, gate, offs, pos1, pos2,
         load_x(0, 768, 512)
         load_x(0, 1280, 256)
         nc.sync.dma_start(offs_t[:], offs)
-        load_x(1, 0, 768)
-        for i in range(4):
-            load_scales(i)
-        load_x(1, 768, 768)
-        for i in range(4, 8):
-            load_scales(i)
-        load_w(0, 4)
-        load_w(4, 4)
+        load_x(1, 0, 512)
+        load_x(1, 512, 512)
+        load_x(1, 1024, 512)
         nc.sync.dma_start(out=bias[:], in_=b)
-        load_w(8, 8)
+        for i in range(8):
+            load_scales(i)
+        for i in range(6):
+            load_w(4 * i, 4)
         nc.sync.dma_start(pos1_t[:], pos1)
         nc.sync.dma_start(pos2_t[:], pos2)
-        load_w(16, 8)
         nc.sync.dma_start(out=gates[:], in_=gate.rearrange("r p t -> p r t"))
 
         grouped = [keep.tile([P, T, 4], BF16, name=f"grouped{a}", align_bytes=64) for a in range(2)]
-        for a in range(2):
+
+        def interleave(a):
             t0 = 0
             for n, eng in X_COPIES[a]:
                 l0, ln, raw = [r for r in raw_of[a] if r[0] <= t0 < r[0] + r[1]][0]
-                src = raw[:, :, t0 - l0 : t0 - l0 + n].rearrange("p j t -> p t j")
+                src = raw[:, :, t0 - l0 : t0 - l0 + n].rearrange("p j (c i) -> p c j i", i=4)
+                dst = grouped[a][:, t0 : t0 + n, :].rearrange("p (c i) j -> p c j i", i=4)
                 if eng == "v":
-                    nc.vector.tensor_copy(out=grouped[a][:, t0 : t0 + n, :], in_=src)
+                    nc.vector.tensor_copy(out=dst, in_=src)
                 else:
-                    nc.scalar.copy(out=grouped[a][:, t0 : t0 + n, :], in_=src)
+                    nc.scalar.copy(out=dst, in_=src)
                 t0 += n
 
         def quantise(a):
@@ -126,11 +126,13 @@ def tile_routed_moe_kernel(tc, xT, w_words, w_scales, b, gate, offs, pos1, pos2,
         def gather(dst, src, s0, n):
             nc.vector.tensor_copy(dst[:, s0 : s0 + n], src[:].indirect(offs_t[:, s0 // 16 : (s0 + n) // 16]))
 
+        interleave(0)
         quantise(0)
         s0 = 0
         for n in WORD0:
             gather(g_codes[0], codes[0], s0, n)
             s0 += n
+        interleave(1)
         quantise(1)
 
         done = {"b": 0, "w": 0}
@@ -164,32 +166,36 @@ def tile_routed_moe_kernel(tc, xT, w_words, w_scales, b, gate, offs, pos1, pos2,
                     nc.scalar.activation(relu[:, cols], acc, Relu, bias=bias[:, e : e + 1])
                     if e == E - 2:
                         nc.scalar.activation(ys[:, cols], relu[:, cols], Square)
-            for c0 in range(s0, s0 + n, 512):
-                c1 = min(c0 + 512, s0 + n)
-                if s0 + n == S:
-                    continue
-                nc.scalar.activation(ys[:, c0:c1], relu[:, c0:c1], Square)
+            if s0 + n < S:
+                step = 512 if s0 < 20 * C else C
+                for c0 in range(s0, s0 + n, step):
+                    cols = slice(c0, c0 + step)
+                    if c0 // 512 in (1, 3, 5):
+                        nc.gpsimd.tensor_tensor(ys[:, cols], relu[:, cols], relu[:, cols], mult)
+                    else:
+                        nc.scalar.activation(ys[:, cols], relu[:, cols], Square)
 
-        t0 = 0
-        for i, (n, how, stores) in enumerate(COMBINE):
-            parts = []
-            for r, pos in enumerate((pos1_t, pos2_t)):
-                part = keep.tile([P, n], F32, name=f"part{i}_{r}")
-                nc.vector.tensor_tensor(
-                    part[:], ys[:].indirect(pos[:, t0 // 16 : (t0 + n) // 16]), gates[:, r, t0 : t0 + n], mult
-                )
-                parts.append(part)
-            if how == "pe":
-                both = psum.tile([P, n], F32, name=f"both{i}")
-                for r in range(2):
-                    nc.tensor.matmul(both[:], ident[:], parts[r][:], start=(r == 0), stop=(r == 1))
-            u0 = 0
-            for k, m in enumerate(stores):
-                total = keep.tile([P, m], F32, name=f"total{i}_{k}")
-                if how == "pe":
-                    nc.scalar.copy(out=total[:], in_=both[:, u0 : u0 + m])
-                else:
-                    nc.vector.tensor_tensor(total[:], parts[0][:, u0 : u0 + m], parts[1][:, u0 : u0 + m], add)
-                nc.sync.dma_start(out=out[:, t0 + u0 : t0 + u0 + m], in_=total[:])
-                u0 += m
+        def fetch(r, t0, n):
+            part = keep.tile([P, n], F32, name=f"part{r}_{t0}")
+            pos = (pos1_t, pos2_t)[r]
+            nc.vector.tensor_tensor(
+                part[:], ys[:].indirect(pos[:, t0 // 16 : (t0 + n) // 16]), gates[:, r, t0 : t0 + n], mult
+            )
+            return part
+
+        parts = [fetch(r, 0, PE_TOKENS) for r in range(2)]
+        both = psum.tile([P, PE_TOKENS], F32, name="both")
+        for r in range(2):
+            nc.tensor.matmul(both[:], ident[:], parts[r][:], start=(r == 0), stop=(r == 1))
+        total = keep.tile([P, PE_TOKENS], F32, name="total")
+        nc.scalar.copy(out=total[:], in_=both[:])
+        nc.sync.dma_start(out=out[:, 0:PE_TOKENS], in_=total[:])
+
+        one = fetch(0, PE_TOKENS, T - PE_TOKENS)
+        t0 = PE_TOKENS
+        for n in COMBINE:
+            two = fetch(1, t0, n)
+            total = keep.tile([P, n], F32, name=f"total{t0}")
+            nc.vector.tensor_tensor(total[:], one[:, t0 - PE_TOKENS : t0 - PE_TOKENS + n], two[:], add)
+            nc.sync.dma_start(out=out[:, t0 : t0 + n], in_=total[:])
             t0 += n

@@ -30,8 +30,10 @@ X_COPIES = [
 X_QUANT = [[512, 512, 256, 256], [512, 512, 512]]
 WORD0 = [1024, 1024, 1024]
 STEPS = [
-    ("b", 512), ("w", 512), ("b", 512), ("w", 512), ("b", 1024), ("w", 1024), ("b", 512), ("w", 512), ("b", 512), ("w", 256), ("w", 256),
+    ("b", 1024), ("w", 512), ("w", 512), ("b", 1024), ("w", 512), ("w", 512), ("b", 512), ("w", 512), ("b", 512), ("w", 256), ("w", 256),
 ]
+BANKS = 6
+ON_VECTOR = (22, 23)
 PE_TOKENS = 512
 COMBINE = [640, 384]
 
@@ -90,10 +92,14 @@ def tile_routed_moe_kernel(tc, xT, w_words, w_scales, b, gate, offs, pos1, pos2,
         load_x(1, 0, 512)
         load_x(1, 512, 512)
         load_x(1, 1024, 512)
-        nc.sync.dma_start(out=bias[:], in_=b)
-        for i in range(8):
+        for i in range(5):
             load_scales(i)
-        for i in range(6):
+        load_w(0, 4)
+        load_w(4, 4)
+        for i in range(5, 8):
+            load_scales(i)
+        nc.sync.dma_start(out=bias[:], in_=b)
+        for i in range(2, 6):
             load_w(4 * i, 4)
         nc.sync.dma_start(pos1_t[:], pos1)
         nc.sync.dma_start(pos2_t[:], pos2)
@@ -136,7 +142,7 @@ def tile_routed_moe_kernel(tc, xT, w_words, w_scales, b, gate, offs, pos1, pos2,
         quantise(1)
 
         done = {"b": 0, "w": 0}
-        banks = {}
+        banks = [psum.tile([P, 4 * C], F32, name=f"bank{i}") for i in range(BANKS)]
         for sort, n in STEPS:
             s0 = done[sort]
             done[sort] += n
@@ -146,9 +152,7 @@ def tile_routed_moe_kernel(tc, xT, w_words, w_scales, b, gate, offs, pos1, pos2,
             gather(g_codes[1], codes[1], s0, n)
             for e in range(s0 // C, (s0 + n) // C):
                 cols = slice(e * C, (e + 1) * C)
-                if e % 4 == 0:
-                    banks[e // 4] = psum.tile([P, 4 * C], F32, name=f"bank{e // 4}")
-                acc = banks[e // 4][:, (e % 4) * C : (e % 4 + 1) * C]
+                acc = banks[e % BANKS][:, e // BANKS * C : (e // BANKS + 1) * C]
                 for a in range(2):
                     nc.tensor.matmul_mx(
                         out=acc,
@@ -159,21 +163,16 @@ def tile_routed_moe_kernel(tc, xT, w_words, w_scales, b, gate, offs, pos1, pos2,
                         start=(a == 0),
                         stop=(a == 1),
                     )
-                if e == E - 1:
+                if e in ON_VECTOR:
                     nc.vector.tensor_scalar(relu[:, cols], acc, bias[:, e : e + 1], 0.0, add, Max)
-                    nc.vector.tensor_tensor(ys[:, cols], relu[:, cols], relu[:, cols], mult)
                 else:
                     nc.scalar.activation(relu[:, cols], acc, Relu, bias=bias[:, e : e + 1])
-                    if e == E - 2:
-                        nc.scalar.activation(ys[:, cols], relu[:, cols], Square)
-            if s0 + n < S:
-                step = 512 if s0 < 20 * C else C
-                for c0 in range(s0, s0 + n, step):
-                    cols = slice(c0, c0 + step)
-                    if c0 // 512 in (1, 3, 5):
-                        nc.gpsimd.tensor_tensor(ys[:, cols], relu[:, cols], relu[:, cols], mult)
-                    else:
-                        nc.scalar.activation(ys[:, cols], relu[:, cols], Square)
+            on_vector = s0 // C in ON_VECTOR
+            step = n if on_vector else (512 if s0 < 16 * C else C)
+            for c0 in range(s0, s0 + n, step):
+                cols = slice(c0, c0 + step)
+                square = nc.vector if on_vector else nc.gpsimd
+                square.tensor_tensor(ys[:, cols], relu[:, cols], relu[:, cols], mult)
 
         def fetch(r, t0, n):
             part = keep.tile([P, n], F32, name=f"part{r}_{t0}")

from contextlib import ExitStack

import concourse.mybir as mybir
from concourse.masks import make_identity

FLOPS = 805306368

F32 = mybir.dt.float32
BF16 = mybir.dt.bfloat16
I32 = mybir.dt.int32
U32 = mybir.dt.uint32
U16 = mybir.dt.uint16
U8 = mybir.dt.uint8
FP8X4 = mybir.dt.float8_e4m3fn_x4
Relu = mybir.ActivationFunctionType.Relu
Square = mybir.ActivationFunctionType.Square
mult = mybir.AluOpType.mult
add = mybir.AluOpType.add
Max = mybir.AluOpType.max

P = 128
T = 1536
E = 24
C = 128
S = E * C
X_COPIES = [
    [(256, "v"), (256, "s"), (256, "v"), (320, "v"), (192, "s"), (160, "v"), (96, "s")],
    [(512, "s"), (512, "s"), (320, "s"), (192, "v")],
]
X_QUANT = [[512, 512, 256, 256], [512, 512, 512]]
WORD0 = [1024, 1024, 1024]
STEPS = [
    ("b", 1024), ("w", 512), ("w", 512), ("b", 1024), ("w", 512), ("w", 512), ("b", 512), ("w", 512), ("b", 512), ("w", 256), ("w", 256),
]
BANKS = 6
ON_VECTOR = (22, 23)
PE_TOKENS = 512
COMBINE = [640, 384]


def tile_routed_moe_kernel(tc, xT, w_words, w_scales, b, gate, offs, pos1, pos2, out):
    nc = tc.nc
    with ExitStack() as ctx:
        keep = ctx.enter_context(tc.tile_pool(name="keep", bufs=1))
        psum = ctx.enter_context(tc.psum_pool(name="psum", bufs=1))

        offs_t = keep.tile([P, S // 16], U16, name="offs_t")
        pos1_t = keep.tile([P, T // 16], U16, name="pos1_t")
        pos2_t = keep.tile([P, T // 16], U16, name="pos2_t")
        codes = [keep.tile([P, T], U32, name=f"codes{a}", align_bytes=64) for a in range(2)]
        scales = keep.tile([P, T], U8, name="scales", align_bytes=64)
        g_codes = [keep.tile([P, S], U32, name=f"g_codes{a}", align_bytes=64) for a in range(2)]
        g_scales = keep.tile([P, S], U8, name="g_scales", align_bytes=64)
        w_codes = keep.tile([P, E, 2, C], U32, name="w_codes", align_bytes=64)
        w_planes = keep.tile([P, S], U8, name="w_planes", align_bytes=64)
        bias = keep.tile([P, E], F32, name="bias")
        relu = keep.tile([P, S], F32, name="relu")
        ys = keep.tile([P, S], F32, name="ys")
        gates = keep.tile([P, 2, T], F32, name="gates")

        nc.gpsimd.memset(scales[:], 0)
        nc.gpsimd.memset(w_planes[:].bitcast(I32), 0)
        ident = keep.tile([P, P], F32, name="ident")
        make_identity(nc, ident[:])

        x_view = xT.rearrange("(a p j) t -> a p j t", p=P, j=4)
        raw_of = [[], []]

        def load_x(a, t0, n):
            raw = keep.tile([P, 4, n], F32, name=f"raw{a}_{t0}")
            nc.sync.dma_start(out=raw[:], in_=x_view[a, :, :, t0 : t0 + n])
            raw_of[a].append((t0, n, raw))

        def load_scales(i):
            a, q = i // 4, i % 4
            row = 32 * q + 4 * a
            nc.sync.dma_start(
                out=w_planes[row : row + 4, :].bitcast(I32).rearrange("q (e n) -> q e n", e=E),
                in_=w_scales[:, a, 4 * q : 4 * q + 4, :].rearrange("e q n -> q e n").bitcast(I32),
            )

        def load_w(e0, n):
            nc.sync.dma_start(
                out=w_codes[:, e0 : e0 + n, :, :].bitcast(I32),
                in_=w_words[e0 : e0 + n].rearrange("e a p n r -> p e a (n r)").bitcast(I32),
            )

        load_x(0, 0, 768)
        load_x(0, 768, 512)
        load_x(0, 1280, 256)
        nc.sync.dma_start(offs_t[:], offs)
        load_x(1, 0, 512)
        load_x(1, 512, 512)
        load_x(1, 1024, 512)
        for i in range(5):
            load_scales(i)
        load_w(0, 4)
        load_w(4, 4)
        for i in range(5, 8):
            load_scales(i)
        nc.sync.dma_start(out=bias[:], in_=b)
        for i in range(2, 6):
            load_w(4 * i, 4)
        nc.sync.dma_start(pos1_t[:], pos1)
        nc.sync.dma_start(pos2_t[:], pos2)
        nc.sync.dma_start(out=gates[:], in_=gate.rearrange("r p t -> p r t"))

        grouped = [keep.tile([P, T, 4], BF16, name=f"grouped{a}", align_bytes=64) for a in range(2)]

        def interleave(a):
            t0 = 0
            for n, eng in X_COPIES[a]:
                l0, ln, raw = [r for r in raw_of[a] if r[0] <= t0 < r[0] + r[1]][0]
                src = raw[:, :, t0 - l0 : t0 - l0 + n].rearrange("p j (c i) -> p c j i", i=4)
                dst = grouped[a][:, t0 : t0 + n, :].rearrange("p (c i) j -> p c j i", i=4)
                if eng == "v":
                    nc.vector.tensor_copy(out=dst, in_=src)
                else:
                    nc.scalar.copy(out=dst, in_=src)
                t0 += n

        def quantise(a):
            t0 = 0
            for n in X_QUANT[a]:
                nc.vector.quantize_mx(
                    out=codes[a][:, t0 : t0 + n].bitcast(FP8X4),
                    scales=scales[4 * a : P, t0 : t0 + n],
                    in_=grouped[a][:, t0 : t0 + n, :].rearrange("p t j -> p (t j)"),
                )
                t0 += n

        def gather(dst, src, s0, n):
            nc.vector.tensor_copy(dst[:, s0 : s0 + n], src[:].indirect(offs_t[:, s0 // 16 : (s0 + n) // 16]))

        interleave(0)
        quantise(0)
        s0 = 0
        for n in WORD0:
            gather(g_codes[0], codes[0], s0, n)
            s0 += n
        interleave(1)
        quantise(1)

        done = {"b": 0, "w": 0}
        banks = [psum.tile([P, 4 * C], F32, name=f"bank{i}") for i in range(BANKS)]
        for sort, n in STEPS:
            s0 = done[sort]
            done[sort] += n
            if sort == "b":
                gather(g_scales, scales, s0, n)
                continue
            gather(g_codes[1], codes[1], s0, n)
            for e in range(s0 // C, (s0 + n) // C):
                cols = slice(e * C, (e + 1) * C)
                acc = banks[e % BANKS][:, e // BANKS * C : (e // BANKS + 1) * C]
                for a in range(2):
                    nc.tensor.matmul_mx(
                        out=acc,
                        lhsT=w_codes[:, e, a, :].bitcast(FP8X4),
                        lhsT_scale=w_planes[4 * a : P, cols],
                        rhs=g_codes[a][:, cols].bitcast(FP8X4),
                        rhs_scale=g_scales[4 * a : P, cols],
                        start=(a == 0),
                        stop=(a == 1),
                    )
                if e in ON_VECTOR:
                    nc.vector.tensor_scalar(relu[:, cols], acc, bias[:, e : e + 1], 0.0, add, Max)
                else:
                    nc.scalar.activation(relu[:, cols], acc, Relu, bias=bias[:, e : e + 1])
            on_vector = s0 // C in ON_VECTOR
            step = n if on_vector else (512 if s0 < 16 * C else C)
            for c0 in range(s0, s0 + n, step):
                cols = slice(c0, c0 + step)
                square = nc.vector if on_vector else nc.gpsimd
                square.tensor_tensor(ys[:, cols], relu[:, cols], relu[:, cols], mult)

        def fetch(r, t0, n):
            part = keep.tile([P, n], F32, name=f"part{r}_{t0}")
            pos = (pos1_t, pos2_t)[r]
            nc.vector.tensor_tensor(
                part[:], ys[:].indirect(pos[:, t0 // 16 : (t0 + n) // 16]), gates[:, r, t0 : t0 + n], mult
            )
            return part

        parts = [fetch(r, 0, PE_TOKENS) for r in range(2)]
        both = psum.tile([P, PE_TOKENS], F32, name="both")
        for r in range(2):
            nc.tensor.matmul(both[:], ident[:], parts[r][:], start=(r == 0), stop=(r == 1))
        total = keep.tile([P, PE_TOKENS], F32, name="total")
        nc.scalar.copy(out=total[:], in_=both[:])
        nc.sync.dma_start(out=out[:, 0:PE_TOKENS], in_=total[:])

        one = fetch(0, PE_TOKENS, T - PE_TOKENS)
        t0 = PE_TOKENS
        for n in COMBINE:
            two = fetch(1, t0, n)
            total = keep.tile([P, n], F32, name=f"total{t0}")
            nc.vector.tensor_tensor(total[:], one[:, t0 - PE_TOKENS : t0 - PE_TOKENS + n], two[:], add)
            nc.sync.dma_start(out=out[:, t0 : t0 + n], in_=total[:])
            t0 += n
